import numpy as np
import ml_dtypes


def mxq(x, axis, fmt="e4m3"):
    dtype, down = {"e4m3": (ml_dtypes.float8_e4m3fn, 7), "e5m2": (ml_dtypes.float8_e5m2, 14)}[fmt]
    v = np.moveaxis(np.asarray(x, np.float32).astype(ml_dtypes.bfloat16).astype(np.float64), axis, -1)
    blocks = v.reshape(v.shape[:-1] + (-1, 32))
    amax = np.abs(blocks).max(-1, keepdims=True)
    byte = np.maximum(np.where(amax > 0, np.frexp(amax)[1] - 1 + 127, 0) - down, 1)
    scale = np.exp2(byte - 127.0)
    codes = (blocks / scale).astype(np.float32).astype(dtype).astype(np.float64)
    return np.moveaxis((codes * scale).reshape(v.shape), -1, axis)


WIDE = False


def mx_kscale(k):
    if not WIDE:
        return np.ones(k)
    levels = np.array([30, -30])
    if k % 512:
        return np.exp2(np.random.permutation(np.resize(levels, k // 32))).repeat(32)
    a = np.empty((k // 512, 16))
    for p in range(k // 512):
        a[p, :8] = np.random.permutation(np.resize(levels, 8))
        for g in range(8):
            far = levels[np.abs(levels - a[p, g]) >= 10]
            a[p, g + 8] = far[np.random.randint(len(far))]
    return np.exp2(a.ravel()).repeat(32)


def f64(x):
    return np.asarray(x).astype(np.float64)


def striped(idx):
    return np.tile(np.asarray(idx).reshape(-1, 16).T, (8, 1)).astype(np.uint16)


def unstriped(offs):
    return offs[:16].T.reshape(-1).astype(np.int64)


E2M1 = np.array([0.0, 0.5, 1.0, 1.5, 2.0, 3.0, 4.0, 6.0, -0.0, -0.5, -1.0, -1.5, -2.0, -3.0, -4.0, -6.0])


def pack_weight(w, fmt):
    k, n = w.shape
    w = f64(np.asarray(w, np.float32).astype(ml_dtypes.bfloat16)).reshape(k // 32, 32, n)
    amax = np.abs(w).max(1)
    if fmt == "e4m3":
        byte = np.frexp(amax)[1] - 1 + 127 - 7
    else:
        mant, ex = np.frexp(amax / 6.0)
        byte = np.where(mant > 0.5, ex, ex - 1) + 127
    byte = np.clip(np.where(amax > 0, byte, 1), 1, 254)
    scaled = (w * np.exp2(127.0 - byte)[:, None, :]).reshape(k, n).astype(np.float32)
    by_word = np.ascontiguousarray(scaled.reshape(k // 512, 128, 4, n).transpose(0, 1, 3, 2))
    if fmt == "e4m3":
        words = by_word.astype(ml_dtypes.float8_e4m3fn).view(np.uint8)
    else:
        c = by_word.astype(ml_dtypes.float4_e2m1fn).view(np.uint8) & 0xF
        words = (c[..., 0::2] | (c[..., 1::2] << 4)).reshape(k // 512, 128, 2 * n)
    return np.ascontiguousarray(words), np.ascontiguousarray(byte.astype(np.uint8).reshape(k // 512, 16, n))


def unpack_weight(words, scales, fmt):
    g, _, n = scales.shape
    words = np.ascontiguousarray(words).reshape(g, 128, n, -1)
    if fmt == "e4m3":
        vals = words.view(ml_dtypes.float8_e4m3fn).astype(np.float64)
    else:
        nib = np.empty((g, 128, n, 4), np.uint8)
        nib[..., 0::2] = words & 0xF
        nib[..., 1::2] = words >> 4
        vals = E2M1[nib]
    vals = vals * np.repeat(np.exp2(scales.astype(np.float64) - 127.0), 8, axis=1)[..., None]
    return vals.transpose(0, 1, 3, 2).reshape(g * 512, n)


K, T, J, R, X, V, O, N, E = 512, 1024, 256, 512, 512, 512, 128, 256, 1024


def setup_inputs():
    n = np.random.standard_normal
    idx = np.random.permutation(T)[:J]
    idx2 = np.random.permutation(X)[:O]
    idx3 = np.random.permutation(V)[:O]
    idx4 = np.random.permutation(J)[:O]
    idx5 = np.random.permutation(T)[:O]
    idx6 = np.random.permutation(E)[:O]
    fk = mx_kscale(K)
    fr = mx_kscale(R)
    xtp = pack_weight(n((K, T)) / fk[:, None], "e2m1")
    wp = pack_weight(n((K, R)) * 1 / np.sqrt(K) * fk[:, None] * fr, "e4m3")
    wbp = pack_weight(n((R, N)) * 1 / np.sqrt(R) / fr[:, None], "e2m1")
    wsp = pack_weight(n((K, N)) * 1 / np.sqrt(K) * fk[:, None], "e4m3")
    return {
        "xt_words": xtp[0],
        "xt_scales": xtp[1],
        "w_words": wp[0],
        "w_scales": wp[1],
        "tb": (n((R, X)) * 0.9).astype(np.float32),
        "tc2": (n((R, V)) * 0.9).astype(np.float32),
        "wb_words": wbp[0],
        "wb_scales": wbp[1],
        "ws_words": wsp[0],
        "ws_scales": wsp[1],
        "offs": striped(idx),
        "offs2": striped(idx2),
        "offs3": striped(idx3),
        "offs4": striped(idx4),
        "offs5": striped(idx5),
        "offs6": striped(idx6),
    }


def reference(xt_words, xt_scales, w_words, w_scales, tb, tc2, wb_words, wb_scales, ws_words, ws_scales, offs, offs2, offs3, offs4, offs5, offs6):
    idx = unstriped(offs)
    idx2 = unstriped(offs2)
    idx3 = unstriped(offs3)
    idx4 = unstriped(offs4)
    idx5 = unstriped(offs5)
    idx6 = unstriped(offs6)
    xtu = unpack_weight(xt_words, xt_scales, "e2m1")
    wu = unpack_weight(w_words, w_scales, "e4m3")
    wbu = unpack_weight(wb_words, wb_scales, "e2m1")
    wsu = unpack_weight(ws_words, ws_scales, "e4m3")
    xtidxg = xtu[:, idx]
    a = wu.T @ xtidxg
    la = a[:, 0:1]
    la2 = a[:, 128:129]
    hid = np.maximum(f64(tb)[:, idx2] * la, f64(tc2)[:, idx3] * la2) - a[:, idx4]
    hidq = mxq(hid, 0, "e5m2")
    xtidx5g = xtu[:, idx5]
    p = wbu.T @ hidq + wsu.T @ xtidx5g
    y = np.zeros((N, E))
    y[:, idx6] = p
    return y

@@ -1,0 +1,181 @@
+from contextlib import ExitStack
+
+import concourse.mybir as mybir
+
+K, T, J, R, X, V, O, N, E = 512, 1024, 256, 512, 512, 512, 128, 256, 1024
+FLOPS = 2 * K * R * J + 2 * R * N * O + 2 * K * N * O
+
+F32 = mybir.dt.float32
+BF16 = mybir.dt.bfloat16
+I32 = mybir.dt.int32
+U32 = mybir.dt.uint32
+U16 = mybir.dt.uint16
+U8 = mybir.dt.uint8
+E4M3X4 = mybir.dt.float8_e4m3fn_x4
+E5M2X4 = mybir.dt.float8_e5m2_x4
+E2M1X4 = mybir.dt.float4_e2m1fn_x4
+COPY = mybir.ActivationFunctionType.Copy
+ALU = mybir.AluOpType
+
+P = 128
+PACK = 4
+
+
+def load_scale_rows(nc, halves, scales):
+    rows = scales.bitcast(I32).rearrange("(h q r) c -> q r h c", h=2, q=2)
+    for q in range(2):
+        nc.sync.dma_start(out=halves[32 * q : 32 * q + 4, :, :], in_=rows[q])
+
+
+def tile_list_twotables_solo_further_scattered_kernel(
+    tc, xt_words, xt_scales, w_words, w_scales, tb, tc2, wb_words, wb_scales, ws_words, ws_scales,
+    offs, offs2, offs3, offs4, offs5, offs6, out,
+):
+    nc = tc.nc
+    with ExitStack() as ctx:
+        sb = ctx.enter_context(tc.tile_pool(name="sb", bufs=1))
+        ps = ctx.enter_context(tc.psum_pool(name="ps", bufs=1))
+
+        l1 = sb.tile([P, J // 16], U16, name="l1")
+        l2 = sb.tile([P, O // 16], U16, name="l2")
+        l3 = sb.tile([P, O // 16], U16, name="l3")
+        l4 = sb.tile([P, O // 16], U16, name="l4")
+        l5 = sb.tile([P, O // 16], U16, name="l5")
+        l6 = sb.tile([P, O // 16], U16, name="l6")
+
+        x_words = sb.tile([P, T], U16, name="x_words", align_bytes=64)
+        x_stage = sb.tile([64, 2, T // 4], I32, name="x_stage", align_bytes=64)
+        x_plane = sb.tile([P, T], U8, name="x_plane", align_bytes=64)
+        w_raw = sb.tile([P, R], U32, name="w_raw", align_bytes=64)
+        w_dealt = sb.tile([P, R], U32, name="w_dealt", align_bytes=64)
+        w_halves = sb.tile([P, 2, R], U8, name="w_halves", align_bytes=64)
+        w_plane = sb.tile([P, R], U8, name="w_plane", align_bytes=64)
+        wb_codes = sb.tile([P, 2 * N], U8, name="wb_codes", align_bytes=64)
+        ws_codes = sb.tile([P, N], U32, name="ws_codes", align_bytes=64)
+        o_plane = sb.tile([P, 2 * N], U8, name="o_plane", align_bytes=64)
+        tb_rows = [sb.tile([P, X], F32, name="tb_rows%d" % t) for t in range(PACK)]
+        tc_rows = [sb.tile([P, V], F32, name="tc_rows%d" % t) for t in range(PACK)]
+        pages = [sb.tile([P, E], F32, name="page%d" % h) for h in range(2)]
+
+        xg_words = sb.tile([P, J], U16, name="xg_words", align_bytes=64)
+        xg_plane = sb.tile([P, J], U8, name="xg_plane", align_bytes=64)
+        xs_words = sb.tile([P, O], U16, name="xs_words", align_bytes=64)
+        xs_plane = sb.tile([P, O], U8, name="xs_plane", align_bytes=64)
+        a_rows = [sb.tile([P, J], F32, name="a_rows%d" % t) for t in range(PACK)]
+        first = sb.tile([P, PACK, O], F32, name="first", align_bytes=64)
+        second = sb.tile([P, PACK, O], F32, name="second", align_bytes=64)
+        larger = sb.tile([P, PACK, O], F32, name="larger", align_bytes=64)
+        picked = sb.tile([P, PACK, O], F32, name="picked", align_bytes=64)
+        hid = sb.tile([P, O * PACK], BF16, name="hid", align_bytes=64)
+        hid_codes = sb.tile([P, O], U32, name="hid_codes", align_bytes=64)
+        hid_plane = sb.tile([P, O], U8, name="hid_plane", align_bytes=64)
+        p_rows = [sb.tile([P, O], F32, name="p_rows%d" % h) for h in range(2)]
+
+        a_banks = [ps.tile([P, J], F32, name="a_bank%d" % t) for t in range(PACK)]
+        p_banks = [ps.tile([P, O], F32, name="p_bank%d" % h) for h in range(2)]
+
+        w_halves32 = w_halves[:].bitcast(I32)
+        o_plane32 = o_plane[:].bitcast(I32)
+        nc.vector.memset(x_stage[:], 0)
+        nc.vector.memset(w_halves32, 0)
+        nc.vector.memset(o_plane32, 0)
+        for h in range(2):
+            nc.vector.memset(pages[h][:], 0.0)
+
+        tb_dealt = tb.rearrange("(p t) x -> t p x", t=PACK)
+        tc_dealt = tc2.rearrange("(p t) x -> t p x", t=PACK)
+
+        nc.sync.dma_start(l1[:], offs)
+        nc.scalar.dma_start(out=x_words[:].bitcast(I32), in_=xt_words[0].bitcast(I32))
+        nc.scalar.dma_start(out=w_raw[:].bitcast(I32), in_=w_words[0].rearrange("p n t -> p (n t)").bitcast(I32))
+        load_scale_rows(nc, x_stage[:], xt_scales[0])
+        load_scale_rows(nc, w_halves32, w_scales[0])
+        nc.sync.dma_start(out=tb_rows[0][:], in_=tb_dealt[0])
+        nc.sync.dma_start(out=tc_rows[0][:], in_=tc_dealt[0])
+        nc.sync.dma_start(out=tb_rows[1][:], in_=tb_dealt[1])
+        nc.sync.dma_start(l2[:], offs2)
+        nc.sync.dma_start(l3[:], offs3)
+        nc.sync.dma_start(l5[:], offs5)
+        nc.sync.dma_start(out=tc_rows[1][:], in_=tc_dealt[1])
+        nc.sync.dma_start(out=tb_rows[2][:], in_=tb_dealt[2])
+        nc.sync.dma_start(l4[:], offs4)
+        nc.sync.dma_start(out=tc_rows[2][:], in_=tc_dealt[2])
+        nc.sync.dma_start(out=tb_rows[3][:], in_=tb_dealt[3])
+        nc.sync.dma_start(out=tc_rows[3][:], in_=tc_dealt[3])
+        nc.sync.dma_start(out=ws_codes[:].bitcast(I32), in_=ws_words[0].rearrange("p n t -> p (n t)").bitcast(I32))
+        nc.sync.dma_start(out=wb_codes[:].bitcast(I32), in_=wb_words[0].bitcast(I32))
+        for q in range(4):
+            nc.sync.dma_start(out=o_plane32[32 * q : 32 * q + 4, N // 4 :], in_=ws_scales[0].bitcast(I32)[4 * q : 4 * q + 4, :])
+        nc.sync.dma_start(l6[:], offs6)
+        for q in range(4):
+            nc.gpsimd.dma_start(out=o_plane32[32 * q : 32 * q + 4, : N // 4], in_=wb_scales[0].bitcast(I32)[4 * q : 4 * q + 4, :])
+
+        x_plane32 = x_plane[:].bitcast(I32)
+        nc.vector.tensor_copy(out=x_plane32[0:64, :], in_=x_stage[:, 0, :])
+        nc.vector.tensor_copy(out=x_plane32[64:128, :], in_=x_stage[:, 1, :])
+        nc.vector.tensor_copy(out=w_halves32[64:128, 0, :], in_=w_halves32[0:64, 1, :])
+        nc.scalar.copy(
+            out=w_dealt[:].rearrange("p (t c i) -> p c t i", t=PACK, i=4),
+            in_=w_raw[:].rearrange("p (c i t) -> p c t i", t=PACK, i=4),
+        )
+        nc.vector.tensor_copy(xg_plane[:], x_plane[:].indirect(l1[:]))
+        nc.vector.tensor_copy(
+            out=w_plane[:].rearrange("p (t c i) -> p c t i", t=PACK, i=16),
+            in_=w_halves[:, 0, :].rearrange("p (c i t) -> p c t i", t=PACK, i=16),
+        )
+        nc.vector.tensor_copy(xg_words[:], x_words[:].indirect(l1[:]))
+
+        for t in range(PACK):
+            cols = slice(P * t, P * (t + 1))
+            nc.tensor.matmul_mx(
+                out=a_banks[t][:],
+                lhsT=w_dealt[:, cols].bitcast(E4M3X4), lhsT_scale=w_plane[:, cols],
+                rhs=xg_words[:].bitcast(E2M1X4), rhs_scale=xg_plane[:],
+                start=True, stop=True,
+            )
+
+        nc.vector.tensor_copy(xs_plane[:], x_plane[:].indirect(l5[:]))
+        nc.vector.tensor_copy(xs_words[:], x_words[:].indirect(l5[:]))
+        for t in range(PACK):
+            if t == 0:
+                nc.scalar.copy(out=a_rows[t][:], in_=a_banks[t][:])
+            else:
+                nc.vector.tensor_copy(out=a_rows[t][:], in_=a_banks[t][:])
+        for t in range(PACK):
+            nc.scalar.activation(out=first[:, t, :], in_=tb_rows[t][:].indirect(l2[:]), func=COPY, scale=a_rows[t][:, 0:1])
+            nc.scalar.activation(out=second[:, t, :], in_=tc_rows[t][:].indirect(l3[:]), func=COPY, scale=a_rows[t][:, 128:129])
+        for t in range(PACK):
+            nc.vector.tensor_copy(picked[:, t, :], a_rows[t][:].indirect(l4[:]))
+        for t in range(PACK):
+            nc.vector.tensor_tensor(larger[:, t, :], first[:, t, :], second[:, t, :], ALU.max)
+        nc.vector.tensor_tensor(
+            hid[:].rearrange("p (c i t) -> p c t i", t=PACK, i=2),
+            larger[:].rearrange("p t (c i) -> p c t i", i=2),
+            picked[:].rearrange("p t (c i) -> p c t i", i=2),
+            ALU.subtract,
+        )
+        nc.vector.quantize_mx(out=hid_codes[:].bitcast(E5M2X4), scales=hid_plane[:], in_=hid[:])
+
+        for h in range(2):
+            nc.tensor.matmul_mx(
+                out=p_banks[h][:],
+                lhsT=ws_codes[:, P * h : P * (h + 1)].bitcast(E4M3X4),
+                lhsT_scale=o_plane[:, N + P * h : N + P * (h + 1)],
+                rhs=xs_words[:].bitcast(E2M1X4), rhs_scale=xs_plane[:],
+                start=True, stop=False,
+            )
+        for h in range(2):
+            nc.tensor.matmul_mx(
+                out=p_banks[h][:],
+                lhsT=wb_codes[:, 2 * P * h : 2 * P * (h + 1)].bitcast(E2M1X4),
+                lhsT_scale=o_plane[:, P * h : P * (h + 1)],
+                rhs=hid_codes[:].bitcast(E5M2X4), rhs_scale=hid_plane[:],
+                start=False, stop=True,
+            )
+
+        nc.vector.tensor_copy(out=p_rows[0][:], in_=p_banks[0][:])
+        nc.scalar.copy(out=p_rows[1][:], in_=p_banks[1][:])
+        nc.vector.tensor_copy(pages[0][:].indirect(l6[:]), p_rows[0][:])
+        nc.scalar.activation(out=pages[1][:].indirect(l6[:]), in_=p_rows[1][:], func=COPY)
+        nc.sync.dma_start(out=out[0:P, :], in_=pages[0][:])
+        nc.scalar.dma_start(out=out[P : 2 * P, :], in_=pages[1][:])

@@ -21,12 +21,6 @@ P = 128
 PACK = 4
 
 
-def load_scale_rows(nc, halves, scales):
-    rows = scales.bitcast(I32).rearrange("(h q r) c -> q r h c", h=2, q=2)
-    for q in range(2):
-        nc.sync.dma_start(out=halves[32 * q : 32 * q + 4, :, :], in_=rows[q])
-
-
 def tile_list_twotables_solo_further_scattered_kernel(
     tc, xt_words, xt_scales, w_words, w_scales, tb, tc2, wb_words, wb_scales, ws_words, ws_scales,
     offs, offs2, offs3, offs4, offs5, offs6, out,
@@ -44,11 +38,10 @@ def tile_list_twotables_solo_further_scattered_kernel(
         l6 = sb.tile([P, O // 16], U16, name="l6")
 
         x_words = sb.tile([P, T], U16, name="x_words", align_bytes=64)
-        x_stage = sb.tile([64, 2, T // 4], I32, name="x_stage", align_bytes=64)
         x_plane = sb.tile([P, T], U8, name="x_plane", align_bytes=64)
         w_raw = sb.tile([P, R], U32, name="w_raw", align_bytes=64)
         w_dealt = sb.tile([P, R], U32, name="w_dealt", align_bytes=64)
-        w_halves = sb.tile([P, 2, R], U8, name="w_halves", align_bytes=64)
+        w_slots = sb.tile([P, 4, R], U8, name="w_slots", align_bytes=64)
         w_plane = sb.tile([P, R], U8, name="w_plane", align_bytes=64)
         wb_codes = sb.tile([P, 2 * N], U8, name="wb_codes", align_bytes=64)
         ws_codes = sb.tile([P, N], U32, name="ws_codes", align_bytes=64)
@@ -64,7 +57,7 @@ def tile_list_twotables_solo_further_scattered_kernel(
         a_rows = [sb.tile([P, J], F32, name="a_rows%d" % t) for t in range(PACK)]
         first = sb.tile([P, PACK, O], F32, name="first", align_bytes=64)
         second = sb.tile([P, PACK, O], F32, name="second", align_bytes=64)
-        larger = sb.tile([P, PACK, O], F32, name="larger", align_bytes=64)
+        larger = sb.tile([P, 2, PACK, O // 2], F32, name="larger", align_bytes=64)
         picked = sb.tile([P, PACK, O], F32, name="picked", align_bytes=64)
         hid = sb.tile([P, O * PACK], BF16, name="hid", align_bytes=64)
         hid_codes = sb.tile([P, O], U32, name="hid_codes", align_bytes=64)
@@ -74,10 +67,11 @@ def tile_list_twotables_solo_further_scattered_kernel(
         a_banks = [ps.tile([P, J], F32, name="a_bank%d" % t) for t in range(PACK)]
         p_banks = [ps.tile([P, O], F32, name="p_bank%d" % h) for h in range(2)]
 
-        w_halves32 = w_halves[:].bitcast(I32)
+        w_slots32 = w_slots[:].bitcast(I32)
+        x_plane32 = x_plane[:].bitcast(I32)
         o_plane32 = o_plane[:].bitcast(I32)
-        nc.vector.memset(x_stage[:], 0)
-        nc.vector.memset(w_halves32, 0)
+        nc.vector.memset(w_slots32[:, 0:3:2, :], 0)
+        nc.vector.memset(x_plane32, 0)
         nc.vector.memset(o_plane32, 0)
         for h in range(2):
             nc.vector.memset(pages[h][:], 0.0)
@@ -88,17 +82,18 @@ def tile_list_twotables_solo_further_scattered_kernel(
         nc.sync.dma_start(l1[:], offs)
         nc.scalar.dma_start(out=x_words[:].bitcast(I32), in_=xt_words[0].bitcast(I32))
         nc.scalar.dma_start(out=w_raw[:].bitcast(I32), in_=w_words[0].rearrange("p n t -> p (n t)").bitcast(I32))
-        load_scale_rows(nc, x_stage[:], xt_scales[0])
-        load_scale_rows(nc, w_halves32, w_scales[0])
+        nc.sync.dma_start(out=w_slots32[0:4, :, :], in_=w_scales[0].bitcast(I32).rearrange("(q r) c -> r q c", r=4))
+        for q in range(4):
+            nc.sync.dma_start(out=x_plane32[32 * q : 32 * q + 4, :], in_=xt_scales[0].bitcast(I32)[4 * q : 4 * q + 4, :])
         nc.sync.dma_start(out=tb_rows[0][:], in_=tb_dealt[0])
         nc.sync.dma_start(out=tc_rows[0][:], in_=tc_dealt[0])
         nc.sync.dma_start(out=tb_rows[1][:], in_=tb_dealt[1])
         nc.sync.dma_start(l2[:], offs2)
         nc.sync.dma_start(l3[:], offs3)
         nc.sync.dma_start(l5[:], offs5)
+        nc.sync.dma_start(l4[:], offs4)
         nc.sync.dma_start(out=tc_rows[1][:], in_=tc_dealt[1])
         nc.sync.dma_start(out=tb_rows[2][:], in_=tb_dealt[2])
-        nc.sync.dma_start(l4[:], offs4)
         nc.sync.dma_start(out=tc_rows[2][:], in_=tc_dealt[2])
         nc.sync.dma_start(out=tb_rows[3][:], in_=tb_dealt[3])
         nc.sync.dma_start(out=tc_rows[3][:], in_=tc_dealt[3])
@@ -110,20 +105,18 @@ def tile_list_twotables_solo_further_scattered_kernel(
         for q in range(4):
             nc.gpsimd.dma_start(out=o_plane32[32 * q : 32 * q + 4, : N // 4], in_=wb_scales[0].bitcast(I32)[4 * q : 4 * q + 4, :])
 
-        x_plane32 = x_plane[:].bitcast(I32)
-        nc.vector.tensor_copy(out=x_plane32[0:64, :], in_=x_stage[:, 0, :])
-        nc.vector.tensor_copy(out=x_plane32[64:128, :], in_=x_stage[:, 1, :])
-        nc.vector.tensor_copy(out=w_halves32[64:128, 0, :], in_=w_halves32[0:64, 1, :])
+        nc.vector.tensor_copy(out=w_slots32[32:36, 0:3, :], in_=w_slots32[0:4, 1:4, :])
+        nc.vector.tensor_copy(out=w_slots32[64:128, 0, :], in_=w_slots32[0:64, 2, :])
         nc.scalar.copy(
             out=w_dealt[:].rearrange("p (t c i) -> p c t i", t=PACK, i=4),
             in_=w_raw[:].rearrange("p (c i t) -> p c t i", t=PACK, i=4),
         )
-        nc.vector.tensor_copy(xg_plane[:], x_plane[:].indirect(l1[:]))
         nc.vector.tensor_copy(
             out=w_plane[:].rearrange("p (t c i) -> p c t i", t=PACK, i=16),
-            in_=w_halves[:, 0, :].rearrange("p (c i t) -> p c t i", t=PACK, i=16),
+            in_=w_slots[:, 0, :].rearrange("p (c i t) -> p c t i", t=PACK, i=16),
         )
         nc.vector.tensor_copy(xg_words[:], x_words[:].indirect(l1[:]))
+        nc.vector.tensor_copy(xg_plane[:], x_plane[:].indirect(l1[:]))
 
         for t in range(PACK):
             cols = slice(P * t, P * (t + 1))
@@ -143,18 +136,36 @@ def tile_list_twotables_solo_further_scattered_kernel(
                 nc.vector.tensor_copy(out=a_rows[t][:], in_=a_banks[t][:])
         for t in range(PACK):
             nc.scalar.activation(out=first[:, t, :], in_=tb_rows[t][:].indirect(l2[:]), func=COPY, scale=a_rows[t][:, 0:1])
-            nc.scalar.activation(out=second[:, t, :], in_=tc_rows[t][:].indirect(l3[:]), func=COPY, scale=a_rows[t][:, 128:129])
+            if t < PACK - 1:
+                nc.scalar.activation(out=second[:, t, :], in_=tc_rows[t][:].indirect(l3[:]), func=COPY, scale=a_rows[t][:, 128:129])
+            else:
+                for u in range(2):
+                    nc.scalar.activation(
+                        out=second[:, t, 64 * u : 64 * (u + 1)], in_=tc_rows[t][:].indirect(l3[:, 4 * u : 4 * (u + 1)]),
+                        func=COPY, scale=a_rows[t][:, 128:129],
+                    )
         for t in range(PACK):
             nc.vector.tensor_copy(picked[:, t, :], a_rows[t][:].indirect(l4[:]))
-        for t in range(PACK):
-            nc.vector.tensor_tensor(larger[:, t, :], first[:, t, :], second[:, t, :], ALU.max)
-        nc.vector.tensor_tensor(
-            hid[:].rearrange("p (c i t) -> p c t i", t=PACK, i=2),
-            larger[:].rearrange("p t (c i) -> p c t i", i=2),
-            picked[:].rearrange("p t (c i) -> p c t i", i=2),
-            ALU.subtract,
-        )
-        nc.vector.quantize_mx(out=hid_codes[:].bitcast(E5M2X4), scales=hid_plane[:], in_=hid[:])
+        for t in range(PACK - 1):
+            nc.vector.tensor_tensor(
+                larger[:, :, t, :],
+                first[:, t, :].rearrange("p (u o) -> p u o", u=2),
+                second[:, t, :].rearrange("p (u o) -> p u o", u=2),
+                ALU.max,
+            )
+        for u in range(2):
+            cols = slice(64 * u, 64 * (u + 1))
+            nc.vector.tensor_tensor(larger[:, u, PACK - 1, :], first[:, PACK - 1, cols], second[:, PACK - 1, cols], ALU.max)
+        for u in range(2):
+            nc.vector.tensor_tensor(
+                hid[:, 256 * u : 256 * (u + 1)].rearrange("p (c i t) -> p c t i", t=PACK, i=2),
+                larger[:, u, :, :].rearrange("p t (c i) -> p c t i", i=2),
+                picked[:, :, 64 * u : 64 * (u + 1)].rearrange("p t (c i) -> p c t i", i=2),
+                ALU.subtract,
+            )
+        for u in range(2):
+            cols = slice(64 * u, 64 * (u + 1))
+            nc.vector.quantize_mx(out=hid_codes[:, cols].bitcast(E5M2X4), scales=hid_plane[:, cols], in_=hid[:, 256 * u : 256 * (u + 1)])
 
         for h in range(2):
             nc.tensor.matmul_mx(

@@ -73,26 +73,27 @@ def tile_list_twotables_solo_further_scattered_kernel(
         nc.vector.memset(w_slots32[:, 0:3:2, :], 0)
         nc.vector.memset(x_plane32, 0)
         nc.vector.memset(o_plane32, 0)
-        for h in range(2):
-            nc.vector.memset(pages[h][:], 0.0)
+        nc.vector.memset(pages[0][:, :511], 0.0)
+        nc.vector.memset(pages[0][:, 511:], 0.0)
+        nc.vector.memset(pages[1][:], 0.0)
 
         tb_dealt = tb.rearrange("(p t) x -> t p x", t=PACK)
         tc_dealt = tc2.rearrange("(p t) x -> t p x", t=PACK)
 
         nc.sync.dma_start(l1[:], offs)
         nc.scalar.dma_start(out=x_words[:].bitcast(I32), in_=xt_words[0].bitcast(I32))
-        nc.scalar.dma_start(out=w_raw[:].bitcast(I32), in_=w_words[0].rearrange("p n t -> p (n t)").bitcast(I32))
         nc.sync.dma_start(out=w_slots32[0:4, :, :], in_=w_scales[0].bitcast(I32).rearrange("(q r) c -> r q c", r=4))
         for q in range(4):
             nc.sync.dma_start(out=x_plane32[32 * q : 32 * q + 4, :], in_=xt_scales[0].bitcast(I32)[4 * q : 4 * q + 4, :])
-        nc.sync.dma_start(out=tb_rows[0][:], in_=tb_dealt[0])
+        nc.sync.dma_start(out=w_raw[:].bitcast(I32), in_=w_words[0].rearrange("p n t -> p (n t)").bitcast(I32))
+        nc.sync.dma_start(l5[:], offs5)
+        nc.gpsimd.dma_start(out=tb_rows[0][:], in_=tb_dealt[0])
         nc.sync.dma_start(out=tc_rows[0][:], in_=tc_dealt[0])
         nc.sync.dma_start(out=tb_rows[1][:], in_=tb_dealt[1])
+        nc.sync.dma_start(out=tc_rows[1][:], in_=tc_dealt[1])
         nc.sync.dma_start(l2[:], offs2)
         nc.sync.dma_start(l3[:], offs3)
-        nc.sync.dma_start(l5[:], offs5)
         nc.sync.dma_start(l4[:], offs4)
-        nc.sync.dma_start(out=tc_rows[1][:], in_=tc_dealt[1])
         nc.sync.dma_start(out=tb_rows[2][:], in_=tb_dealt[2])
         nc.sync.dma_start(out=tc_rows[2][:], in_=tc_dealt[2])
         nc.sync.dma_start(out=tb_rows[3][:], in_=tb_dealt[3])

@@ -41,7 +41,7 @@ def tile_list_twotables_solo_further_scattered_kernel(
         x_plane = sb.tile([P, T], U8, name="x_plane", align_bytes=64)
         w_raw = sb.tile([P, R], U32, name="w_raw", align_bytes=64)
         w_dealt = sb.tile([P, R], U32, name="w_dealt", align_bytes=64)
-        w_slots = sb.tile([P, 4, R], U8, name="w_slots", align_bytes=64)
+        w_slots = sb.tile([P, 2, R], U8, name="w_slots", align_bytes=64)
         w_plane = sb.tile([P, R], U8, name="w_plane", align_bytes=64)
         wb_codes = sb.tile([P, 2 * N], U8, name="wb_codes", align_bytes=64)
         ws_codes = sb.tile([P, N], U32, name="ws_codes", align_bytes=64)
@@ -50,11 +50,12 @@ def tile_list_twotables_solo_further_scattered_kernel(
         tc_rows = [sb.tile([P, V], F32, name="tc_rows%d" % t) for t in range(PACK)]
         pages = [sb.tile([P, E], F32, name="page%d" % h) for h in range(2)]
 
-        xg_words = sb.tile([P, J], U16, name="xg_words", align_bytes=64)
-        xg_plane = sb.tile([P, J], U8, name="xg_plane", align_bytes=64)
+        xg_words = [sb.tile([P, P], U16, name="xg_words%d" % u, align_bytes=64) for u in range(2)]
+        xg_plane = [sb.tile([P, P], U8, name="xg_plane%d" % u, align_bytes=64) for u in range(2)]
         xs_words = sb.tile([P, O], U16, name="xs_words", align_bytes=64)
         xs_plane = sb.tile([P, O], U8, name="xs_plane", align_bytes=64)
-        a_rows = [sb.tile([P, J], F32, name="a_rows%d" % t) for t in range(PACK)]
+        a_rows = sb.tile([P, PACK, J], F32, name="a_rows", align_bytes=64)
+        lead = [sb.tile([P, PACK], F32, name="lead%d" % u) for u in range(2)]
         first = sb.tile([P, PACK, O], F32, name="first", align_bytes=64)
         second = sb.tile([P, PACK, O], F32, name="second", align_bytes=64)
         larger = sb.tile([P, 2, PACK, O // 2], F32, name="larger", align_bytes=64)
@@ -64,13 +65,13 @@ def tile_list_twotables_solo_further_scattered_kernel(
         hid_plane = sb.tile([P, O], U8, name="hid_plane", align_bytes=64)
         p_rows = [sb.tile([P, O], F32, name="p_rows%d" % h) for h in range(2)]
 
-        a_banks = [ps.tile([P, J], F32, name="a_bank%d" % t) for t in range(PACK)]
+        a_banks = [ps.tile([P, PACK, P], F32, name="a_bank%d" % u) for u in range(2)]
         p_banks = [ps.tile([P, O], F32, name="p_bank%d" % h) for h in range(2)]
 
         w_slots32 = w_slots[:].bitcast(I32)
         x_plane32 = x_plane[:].bitcast(I32)
         o_plane32 = o_plane[:].bitcast(I32)
-        nc.vector.memset(w_slots32[:, 0:3:2, :], 0)
+        nc.vector.memset(w_slots32, 0)
         nc.vector.memset(x_plane32, 0)
         nc.vector.memset(o_plane32, 0)
         nc.vector.memset(pages[0][:, :511], 0.0)
@@ -82,32 +83,32 @@ def tile_list_twotables_solo_further_scattered_kernel(
 
         nc.sync.dma_start(l1[:], offs)
         nc.scalar.dma_start(out=x_words[:].bitcast(I32), in_=xt_words[0].bitcast(I32))
-        nc.sync.dma_start(out=w_slots32[0:4, :, :], in_=w_scales[0].bitcast(I32).rearrange("(q r) c -> r q c", r=4))
+        w_scale_rows = w_scales[0].bitcast(I32).rearrange("(h q r) c -> q r h c", h=2, q=2)
+        for q in range(2):
+            nc.sync.dma_start(out=w_slots32[32 * q : 32 * q + 4, :, :], in_=w_scale_rows[q])
+        nc.sync.dma_start(out=w_raw[:].bitcast(I32), in_=w_words[0].rearrange("p n t -> p (n t)").bitcast(I32))
         for q in range(4):
             nc.sync.dma_start(out=x_plane32[32 * q : 32 * q + 4, :], in_=xt_scales[0].bitcast(I32)[4 * q : 4 * q + 4, :])
-        nc.sync.dma_start(out=w_raw[:].bitcast(I32), in_=w_words[0].rearrange("p n t -> p (n t)").bitcast(I32))
         nc.sync.dma_start(l5[:], offs5)
-        nc.gpsimd.dma_start(out=tb_rows[0][:], in_=tb_dealt[0])
-        nc.sync.dma_start(out=tc_rows[0][:], in_=tc_dealt[0])
-        nc.sync.dma_start(out=tb_rows[1][:], in_=tb_dealt[1])
-        nc.sync.dma_start(out=tc_rows[1][:], in_=tc_dealt[1])
+        for t in range(2):
+            nc.gpsimd.dma_start(out=tb_rows[t][:], in_=tb_dealt[t])
+        for t in range(2, PACK):
+            nc.sync.dma_start(out=tb_rows[t][:], in_=tb_dealt[t])
         nc.sync.dma_start(l2[:], offs2)
         nc.sync.dma_start(l3[:], offs3)
         nc.sync.dma_start(l4[:], offs4)
-        nc.sync.dma_start(out=tb_rows[2][:], in_=tb_dealt[2])
-        nc.sync.dma_start(out=tc_rows[2][:], in_=tc_dealt[2])
-        nc.sync.dma_start(out=tb_rows[3][:], in_=tb_dealt[3])
-        nc.sync.dma_start(out=tc_rows[3][:], in_=tc_dealt[3])
+        for t in range(PACK):
+            nc.sync.dma_start(out=tc_rows[t][:], in_=tc_dealt[t])
         nc.sync.dma_start(out=ws_codes[:].bitcast(I32), in_=ws_words[0].rearrange("p n t -> p (n t)").bitcast(I32))
         nc.sync.dma_start(out=wb_codes[:].bitcast(I32), in_=wb_words[0].bitcast(I32))
         for q in range(4):
             nc.sync.dma_start(out=o_plane32[32 * q : 32 * q + 4, N // 4 :], in_=ws_scales[0].bitcast(I32)[4 * q : 4 * q + 4, :])
-        nc.sync.dma_start(l6[:], offs6)
         for q in range(4):
-            nc.gpsimd.dma_start(out=o_plane32[32 * q : 32 * q + 4, : N // 4], in_=wb_scales[0].bitcast(I32)[4 * q : 4 * q + 4, :])
+            queue = nc.gpsimd if q < 2 else nc.sync
+            queue.dma_start(out=o_plane32[32 * q : 32 * q + 4, : N // 4], in_=wb_scales[0].bitcast(I32)[4 * q : 4 * q + 4, :])
+        nc.sync.dma_start(l6[:], offs6)
 
-        nc.vector.tensor_copy(out=w_slots32[32:36, 0:3, :], in_=w_slots32[0:4, 1:4, :])
-        nc.vector.tensor_copy(out=w_slots32[64:128, 0, :], in_=w_slots32[0:64, 2, :])
+        nc.vector.tensor_copy(out=w_slots32[64:128, 0, :], in_=w_slots32[0:64, 1, :])
         nc.scalar.copy(
             out=w_dealt[:].rearrange("p (t c i) -> p c t i", t=PACK, i=4),
             in_=w_raw[:].rearrange("p (c i t) -> p c t i", t=PACK, i=4),
@@ -116,37 +117,34 @@ def tile_list_twotables_solo_further_scattered_kernel(
             out=w_plane[:].rearrange("p (t c i) -> p c t i", t=PACK, i=16),
             in_=w_slots[:, 0, :].rearrange("p (c i t) -> p c t i", t=PACK, i=16),
         )
-        nc.vector.tensor_copy(xg_words[:], x_words[:].indirect(l1[:]))
-        nc.vector.tensor_copy(xg_plane[:], x_plane[:].indirect(l1[:]))
-
-        for t in range(PACK):
-            cols = slice(P * t, P * (t + 1))
-            nc.tensor.matmul_mx(
-                out=a_banks[t][:],
-                lhsT=w_dealt[:, cols].bitcast(E4M3X4), lhsT_scale=w_plane[:, cols],
-                rhs=xg_words[:].bitcast(E2M1X4), rhs_scale=xg_plane[:],
-                start=True, stop=True,
-            )
+        for u in range(2):
+            nc.vector.tensor_copy(xg_words[u][:], x_words[:].indirect(l1[:, 8 * u : 8 * (u + 1)]))
+            nc.vector.tensor_copy(xg_plane[u][:], x_plane[:].indirect(l1[:, 8 * u : 8 * (u + 1)]))
+            for t in range(PACK):
+                cols = slice(P * t, P * (t + 1))
+                nc.tensor.matmul_mx(
+                    out=a_banks[u][:, t, :],
+                    lhsT=w_dealt[:, cols].bitcast(E4M3X4), lhsT_scale=w_plane[:, cols],
+                    rhs=xg_words[u][:].bitcast(E2M1X4), rhs_scale=xg_plane[u][:],
+                    start=True, stop=True,
+                )
+            nc.scalar.copy(out=lead[u][:], in_=a_banks[u][:, :, 0])
 
         nc.vector.tensor_copy(xs_plane[:], x_plane[:].indirect(l5[:]))
         nc.vector.tensor_copy(xs_words[:], x_words[:].indirect(l5[:]))
+        for u in range(2):
+            nc.vector.tensor_copy(out=a_rows[:, :, P * u : P * (u + 1)], in_=a_banks[u][:])
         for t in range(PACK):
-            if t == 0:
-                nc.scalar.copy(out=a_rows[t][:], in_=a_banks[t][:])
-            else:
-                nc.vector.tensor_copy(out=a_rows[t][:], in_=a_banks[t][:])
+            nc.scalar.activation(out=first[:, t, :], in_=tb_rows[t][:].indirect(l2[:]), func=COPY, scale=lead[0][:, t : t + 1])
+        for t in range(PACK - 1):
+            nc.scalar.activation(out=second[:, t, :], in_=tc_rows[t][:].indirect(l3[:]), func=COPY, scale=lead[1][:, t : t + 1])
+        for u in range(2):
+            nc.scalar.activation(
+                out=second[:, PACK - 1, 64 * u : 64 * (u + 1)], in_=tc_rows[PACK - 1][:].indirect(l3[:, 4 * u : 4 * (u + 1)]),
+                func=COPY, scale=lead[1][:, PACK - 1 : PACK],
+            )
         for t in range(PACK):
-            nc.scalar.activation(out=first[:, t, :], in_=tb_rows[t][:].indirect(l2[:]), func=COPY, scale=a_rows[t][:, 0:1])
-            if t < PACK - 1:
-                nc.scalar.activation(out=second[:, t, :], in_=tc_rows[t][:].indirect(l3[:]), func=COPY, scale=a_rows[t][:, 128:129])
-            else:
-                for u in range(2):
-                    nc.scalar.activation(
-                        out=second[:, t, 64 * u : 64 * (u + 1)], in_=tc_rows[t][:].indirect(l3[:, 4 * u : 4 * (u + 1)]),
-                        func=COPY, scale=a_rows[t][:, 128:129],
-                    )
-        for t in range(PACK):
-            nc.vector.tensor_copy(picked[:, t, :], a_rows[t][:].indirect(l4[:]))
+            nc.vector.tensor_copy(picked[:, t, :], a_rows[:, t, :].indirect(l4[:]))
         for t in range(PACK - 1):
             nc.vector.tensor_tensor(
                 larger[:, :, t, :],

from contextlib import ExitStack

import concourse.mybir as mybir

K, T, J, R, X, V, O, N, E = 512, 1024, 256, 512, 512, 512, 128, 256, 1024
FLOPS = 2 * K * R * J + 2 * R * N * O + 2 * K * N * O

F32 = mybir.dt.float32
BF16 = mybir.dt.bfloat16
I32 = mybir.dt.int32
U32 = mybir.dt.uint32
U16 = mybir.dt.uint16
U8 = mybir.dt.uint8
E4M3X4 = mybir.dt.float8_e4m3fn_x4
E5M2X4 = mybir.dt.float8_e5m2_x4
E2M1X4 = mybir.dt.float4_e2m1fn_x4
COPY = mybir.ActivationFunctionType.Copy
ALU = mybir.AluOpType

P = 128
PACK = 4


def tile_list_twotables_solo_further_scattered_kernel(
    tc, xt_words, xt_scales, w_words, w_scales, tb, tc2, wb_words, wb_scales, ws_words, ws_scales,
    offs, offs2, offs3, offs4, offs5, offs6, out,
):
    nc = tc.nc
    with ExitStack() as ctx:
        sb = ctx.enter_context(tc.tile_pool(name="sb", bufs=1))
        ps = ctx.enter_context(tc.psum_pool(name="ps", bufs=1))

        l1 = sb.tile([P, J // 16], U16, name="l1")
        l2 = sb.tile([P, O // 16], U16, name="l2")
        l3 = sb.tile([P, O // 16], U16, name="l3")
        l4 = sb.tile([P, O // 16], U16, name="l4")
        l5 = sb.tile([P, O // 16], U16, name="l5")
        l6 = sb.tile([P, O // 16], U16, name="l6")

        x_words = sb.tile([P, T], U16, name="x_words", align_bytes=64)
        x_plane = sb.tile([P, T], U8, name="x_plane", align_bytes=64)
        w_raw = sb.tile([P, R], U32, name="w_raw", align_bytes=64)
        w_dealt = sb.tile([P, R], U32, name="w_dealt", align_bytes=64)
        w_slots = sb.tile([P, 2, R], U8, name="w_slots", align_bytes=64)
        w_plane = sb.tile([P, R], U8, name="w_plane", align_bytes=64)
        wb_codes = sb.tile([P, 2 * N], U8, name="wb_codes", align_bytes=64)
        ws_codes = sb.tile([P, N], U32, name="ws_codes", align_bytes=64)
        o_plane = sb.tile([P, 2 * N], U8, name="o_plane", align_bytes=64)
        tb_rows = [sb.tile([P, X], F32, name="tb_rows%d" % t) for t in range(PACK)]
        tc_rows = [sb.tile([P, V], F32, name="tc_rows%d" % t) for t in range(PACK)]
        pages = [sb.tile([P, E], F32, name="page%d" % h) for h in range(2)]

        xg_words = [sb.tile([P, P], U16, name="xg_words%d" % u, align_bytes=64) for u in range(2)]
        xg_plane = [sb.tile([P, P], U8, name="xg_plane%d" % u, align_bytes=64) for u in range(2)]
        xs_words = sb.tile([P, O], U16, name="xs_words", align_bytes=64)
        xs_plane = sb.tile([P, O], U8, name="xs_plane", align_bytes=64)
        a_rows = sb.tile([P, PACK, J], F32, name="a_rows", align_bytes=64)
        lead = [sb.tile([P, PACK], F32, name="lead%d" % u) for u in range(2)]
        first = sb.tile([P, PACK, O], F32, name="first", align_bytes=64)
        second = sb.tile([P, PACK, O], F32, name="second", align_bytes=64)
        larger = sb.tile([P, 2, PACK, O // 2], F32, name="larger", align_bytes=64)
        picked = sb.tile([P, PACK, O], F32, name="picked", align_bytes=64)
        hid = sb.tile([P, O * PACK], BF16, name="hid", align_bytes=64)
        hid_codes = sb.tile([P, O], U32, name="hid_codes", align_bytes=64)
        hid_plane = sb.tile([P, O], U8, name="hid_plane", align_bytes=64)
        p_rows = [sb.tile([P, O], F32, name="p_rows%d" % h) for h in range(2)]

        a_banks = [ps.tile([P, PACK, P], F32, name="a_bank%d" % u) for u in range(2)]
        p_banks = [ps.tile([P, O], F32, name="p_bank%d" % h) for h in range(2)]

        w_slots32 = w_slots[:].bitcast(I32)
        x_plane32 = x_plane[:].bitcast(I32)
        o_plane32 = o_plane[:].bitcast(I32)
        nc.vector.memset(w_slots32, 0)
        nc.vector.memset(x_plane32, 0)
        nc.vector.memset(o_plane32, 0)
        nc.vector.memset(pages[0][:, :511], 0.0)
        nc.vector.memset(pages[0][:, 511:], 0.0)
        nc.vector.memset(pages[1][:], 0.0)

        tb_dealt = tb.rearrange("(p t) x -> t p x", t=PACK)
        tc_dealt = tc2.rearrange("(p t) x -> t p x", t=PACK)

        nc.sync.dma_start(l1[:], offs)
        nc.scalar.dma_start(out=x_words[:].bitcast(I32), in_=xt_words[0].bitcast(I32))
        w_scale_rows = w_scales[0].bitcast(I32).rearrange("(h q r) c -> q r h c", h=2, q=2)
        for q in range(2):
            nc.sync.dma_start(out=w_slots32[32 * q : 32 * q + 4, :, :], in_=w_scale_rows[q])
        nc.sync.dma_start(out=w_raw[:].bitcast(I32), in_=w_words[0].rearrange("p n t -> p (n t)").bitcast(I32))
        for q in range(4):
            nc.sync.dma_start(out=x_plane32[32 * q : 32 * q + 4, :], in_=xt_scales[0].bitcast(I32)[4 * q : 4 * q + 4, :])
        nc.sync.dma_start(l5[:], offs5)
        for t in range(2):
            nc.gpsimd.dma_start(out=tb_rows[t][:], in_=tb_dealt[t])
        for t in range(2, PACK):
            nc.sync.dma_start(out=tb_rows[t][:], in_=tb_dealt[t])
        nc.sync.dma_start(l2[:], offs2)
        nc.sync.dma_start(l3[:], offs3)
        nc.sync.dma_start(l4[:], offs4)
        for t in range(PACK):
            nc.sync.dma_start(out=tc_rows[t][:], in_=tc_dealt[t])
        nc.sync.dma_start(out=ws_codes[:].bitcast(I32), in_=ws_words[0].rearrange("p n t -> p (n t)").bitcast(I32))
        nc.sync.dma_start(out=wb_codes[:].bitcast(I32), in_=wb_words[0].bitcast(I32))
        for q in range(4):
            nc.sync.dma_start(out=o_plane32[32 * q : 32 * q + 4, N // 4 :], in_=ws_scales[0].bitcast(I32)[4 * q : 4 * q + 4, :])
        for q in range(4):
            queue = nc.gpsimd if q < 2 else nc.sync
            queue.dma_start(out=o_plane32[32 * q : 32 * q + 4, : N // 4], in_=wb_scales[0].bitcast(I32)[4 * q : 4 * q + 4, :])
        nc.sync.dma_start(l6[:], offs6)

        nc.vector.tensor_copy(out=w_slots32[64:128, 0, :], in_=w_slots32[0:64, 1, :])
        nc.scalar.copy(
            out=w_dealt[:].rearrange("p (t c i) -> p c t i", t=PACK, i=4),
            in_=w_raw[:].rearrange("p (c i t) -> p c t i", t=PACK, i=4),
        )
        nc.vector.tensor_copy(
            out=w_plane[:].rearrange("p (t c i) -> p c t i", t=PACK, i=16),
            in_=w_slots[:, 0, :].rearrange("p (c i t) -> p c t i", t=PACK, i=16),
        )
        for u in range(2):
            nc.vector.tensor_copy(xg_words[u][:], x_words[:].indirect(l1[:, 8 * u : 8 * (u + 1)]))
            nc.vector.tensor_copy(xg_plane[u][:], x_plane[:].indirect(l1[:, 8 * u : 8 * (u + 1)]))
            for t in range(PACK):
                cols = slice(P * t, P * (t + 1))
                nc.tensor.matmul_mx(
                    out=a_banks[u][:, t, :],
                    lhsT=w_dealt[:, cols].bitcast(E4M3X4), lhsT_scale=w_plane[:, cols],
                    rhs=xg_words[u][:].bitcast(E2M1X4), rhs_scale=xg_plane[u][:],
                    start=True, stop=True,
                )
            nc.scalar.copy(out=lead[u][:], in_=a_banks[u][:, :, 0])

        nc.vector.tensor_copy(xs_plane[:], x_plane[:].indirect(l5[:]))
        nc.vector.tensor_copy(xs_words[:], x_words[:].indirect(l5[:]))
        for u in range(2):
            nc.vector.tensor_copy(out=a_rows[:, :, P * u : P * (u + 1)], in_=a_banks[u][:])
        for t in range(PACK):
            nc.scalar.activation(out=first[:, t, :], in_=tb_rows[t][:].indirect(l2[:]), func=COPY, scale=lead[0][:, t : t + 1])
        for t in range(PACK - 1):
            nc.scalar.activation(out=second[:, t, :], in_=tc_rows[t][:].indirect(l3[:]), func=COPY, scale=lead[1][:, t : t + 1])
        for u in range(2):
            nc.scalar.activation(
                out=second[:, PACK - 1, 64 * u : 64 * (u + 1)], in_=tc_rows[PACK - 1][:].indirect(l3[:, 4 * u : 4 * (u + 1)]),
                func=COPY, scale=lead[1][:, PACK - 1 : PACK],
            )
        for t in range(PACK):
            nc.vector.tensor_copy(picked[:, t, :], a_rows[:, t, :].indirect(l4[:]))
        for t in range(PACK - 1):
            nc.vector.tensor_tensor(
                larger[:, :, t, :],
                first[:, t, :].rearrange("p (u o) -> p u o", u=2),
                second[:, t, :].rearrange("p (u o) -> p u o", u=2),
                ALU.max,
            )
        for u in range(2):
            cols = slice(64 * u, 64 * (u + 1))
            nc.vector.tensor_tensor(larger[:, u, PACK - 1, :], first[:, PACK - 1, cols], second[:, PACK - 1, cols], ALU.max)
        for u in range(2):
            nc.vector.tensor_tensor(
                hid[:, 256 * u : 256 * (u + 1)].rearrange("p (c i t) -> p c t i", t=PACK, i=2),
                larger[:, u, :, :].rearrange("p t (c i) -> p c t i", i=2),
                picked[:, :, 64 * u : 64 * (u + 1)].rearrange("p t (c i) -> p c t i", i=2),
                ALU.subtract,
            )
        for u in range(2):
            cols = slice(64 * u, 64 * (u + 1))
            nc.vector.quantize_mx(out=hid_codes[:, cols].bitcast(E5M2X4), scales=hid_plane[:, cols], in_=hid[:, 256 * u : 256 * (u + 1)])

        for h in range(2):
            nc.tensor.matmul_mx(
                out=p_banks[h][:],
                lhsT=ws_codes[:, P * h : P * (h + 1)].bitcast(E4M3X4),
                lhsT_scale=o_plane[:, N + P * h : N + P * (h + 1)],
                rhs=xs_words[:].bitcast(E2M1X4), rhs_scale=xs_plane[:],
                start=True, stop=False,
            )
        for h in range(2):
            nc.tensor.matmul_mx(
                out=p_banks[h][:],
                lhsT=wb_codes[:, 2 * P * h : 2 * P * (h + 1)].bitcast(E2M1X4),
                lhsT_scale=o_plane[:, P * h : P * (h + 1)],
                rhs=hid_codes[:].bitcast(E5M2X4), rhs_scale=hid_plane[:],
                start=False, stop=True,
            )

        nc.vector.tensor_copy(out=p_rows[0][:], in_=p_banks[0][:])
        nc.scalar.copy(out=p_rows[1][:], in_=p_banks[1][:])
        nc.vector.tensor_copy(pages[0][:].indirect(l6[:]), p_rows[0][:])
        nc.scalar.activation(out=pages[1][:].indirect(l6[:]), in_=p_rows[1][:], func=COPY)
        nc.sync.dma_start(out=out[0:P, :], in_=pages[0][:])
        nc.scalar.dma_start(out=out[P : 2 * P, :], in_=pages[1][:])
